import numpy as np
import ml_dtypes


def mxq(x, axis, fmt="e4m3"):
    dtype, down = {"e4m3": (ml_dtypes.float8_e4m3fn, 7), "e5m2": (ml_dtypes.float8_e5m2, 14)}[fmt]
    v = np.moveaxis(np.asarray(x, np.float32).astype(ml_dtypes.bfloat16).astype(np.float64), axis, -1)
    blocks = v.reshape(v.shape[:-1] + (-1, 32))
    amax = np.abs(blocks).max(-1, keepdims=True)
    byte = np.maximum(np.where(amax > 0, np.frexp(amax)[1] - 1 + 127, 0) - down, 1)
    scale = np.exp2(byte - 127.0)
    codes = (blocks / scale).astype(np.float32).astype(dtype).astype(np.float64)
    return np.moveaxis((codes * scale).reshape(v.shape), -1, axis)


WIDE = False


def mx_kscale(k):
    if not WIDE:
        return np.ones(k)
    levels = np.array([10, -10, 5, -5, 0])
    if k % 512:
        return np.exp2(np.random.permutation(np.resize(levels, k // 32))).repeat(32)
    a = np.empty((k // 512, 16))
    for p in range(k // 512):
        a[p, :8] = np.random.permutation(np.resize(levels, 8))
        for g in range(8):
            far = levels[np.abs(levels - a[p, g]) >= 10]
            a[p, g + 8] = far[np.random.randint(len(far))]
    return np.exp2(a.ravel()).repeat(32)


BF16 = ml_dtypes.bfloat16


def bf(x):
    return np.asarray(x, np.float32).astype(BF16)


def f64(x):
    return np.asarray(x).astype(np.float64)


E2M1 = np.array([0.0, 0.5, 1.0, 1.5, 2.0, 3.0, 4.0, 6.0, -0.0, -0.5, -1.0, -1.5, -2.0, -3.0, -4.0, -6.0])


def pack_weight(w, fmt):
    k, n = w.shape
    w = f64(bf(w)).reshape(k // 32, 32, n)
    amax = np.abs(w).max(1)
    if fmt == "e4m3":
        byte = np.frexp(amax)[1] - 1 + 127 - 7
    else:
        mant, ex = np.frexp(amax / 6.0)
        byte = np.where(mant > 0.5, ex, ex - 1) + 127
    byte = np.clip(np.where(amax > 0, byte, 1), 1, 254)
    scaled = (w * np.exp2(127.0 - byte)[:, None, :]).reshape(k, n).astype(np.float32)
    by_word = np.ascontiguousarray(scaled.reshape(k // 512, 128, 4, n).transpose(0, 1, 3, 2))
    if fmt == "e4m3":
        words = by_word.astype(ml_dtypes.float8_e4m3fn).view(np.uint8)
    else:
        c = by_word.astype(ml_dtypes.float4_e2m1fn).view(np.uint8) & 0xF
        words = c[..., 0::2] | (c[..., 1::2] << 4)
    return np.ascontiguousarray(words), np.ascontiguousarray(byte.astype(np.uint8).reshape(k // 512, 16, n))


def unpack_weight(words, scales, fmt):
    g, p, n, _ = words.shape
    if fmt == "e4m3":
        vals = np.ascontiguousarray(words).view(ml_dtypes.float8_e4m3fn).astype(np.float64)
    else:
        nib = np.empty((g, p, n, 4), np.uint8)
        nib[..., 0::2] = words & 0xF
        nib[..., 1::2] = words >> 4
        vals = E2M1[nib]
    vals = vals * np.repeat(np.exp2(scales.astype(np.float64) - 127.0), 8, axis=1)[..., None]
    return vals.transpose(0, 1, 3, 2).reshape(g * 512, n)
def pack4(w):
    words, scales = pack_weight(w, "e2m1")
    return words.reshape(words.shape[0], 128, -1), scales


def unpack4(words, scales):
    return unpack_weight(words.reshape(words.shape[0], 128, -1, 2), scales, "e2m1")


M, N, R = 1536, 2048, 512


def setup_inputs():
    s, t = mx_kscale(R), mx_kscale(N)
    v_words, v_scales = pack4(np.random.standard_normal((R, N)) / s[:, None] / t)
    return {"u": bf(np.random.standard_normal((M, R)) / np.sqrt(R) * s),
            "v_words": v_words,
            "v_scales": v_scales,
            "c": bf(8.0 * np.random.standard_normal((R, R)) / np.sqrt(R * N) * s[:, None]),
            "y": bf(np.random.standard_normal((M, N)) / t),
            "mask": bf(np.random.uniform(0.1, 1.0, (M, N)) * t * t)}


def reference(u, v_words, v_scales, c, y, mask):
    vt = unpack4(v_words, v_scales)
    pred = mxq(f64(u), 1, "e4m3") @ vt
    z = vt.T @ mxq(f64(c), 0, "e4m3")
    e = f64(mask) * (pred - f64(y))
    return mxq(e, 1, "e4m3") @ mxq(z, 0, "e4m3")

@@ -1,0 +1,335 @@
+from contextlib import ExitStack
+
+import concourse.mybir as mybir
+from concourse.masks import make_identity
+
+M, N, R = 1536, 2048, 512
+FLOPS = 2 * M * N * R + 2 * N * R * R + 2 * M * N * R
+
+F32 = mybir.dt.float32
+BF16 = mybir.dt.bfloat16
+I32 = mybir.dt.int32
+U32 = mybir.dt.uint32
+U8 = mybir.dt.uint8
+FP8X4 = mybir.dt.float8_e4m3fn_x4
+FP4X4 = mybir.dt.float4_e2m1fn_x4
+SUB = mybir.AluOpType.subtract
+MULT = mybir.AluOpType.mult
+
+P = 128
+CHUNK = 512
+TILES = M // P
+CHUNKS = N // CHUNK
+UNIT = 2048
+
+VECTOR_CHUNKS = (1, 2)
+GPSIMD_CHUNKS = (0, 3)
+CHUNK_ORDER = VECTOR_CHUNKS + GPSIMD_CHUNKS
+
+RING_IN = 8
+RING_E = 5
+RING_OUT = 4
+RING_STAGE = 3
+
+TURNS = {
+    1: [("u", 2), ("z", 0)],
+    2: [("u", 4), ("u", 6), ("z", 1)],
+    3: [("z", 2), ("e", 0)],
+    4: [("z", 3), ("e", 1), ("e", 2), ("e", 3)],
+    5: [("e", 4), ("u", 8)],
+    6: [("e", 5), ("u", 10)],
+    7: [("e", 6)],
+    8: [("e", 7)],
+    9: [("e", 8)],
+    10: [("e", 9)],
+    11: [("e", 10)],
+}
+QUANTS = {
+    0: [("c", 0)],
+    1: [("u", 2)],
+    2: [("z", 0)],
+    3: [("z", 1), ("u", 4), ("u", 6)],
+    4: [("z", 2), ("e", 0)],
+    5: [("z", 3), ("e", 1)],
+    6: [("e", 2), ("e", 3)],
+    7: [("e", 4), ("u", 8), ("u", 10)],
+    8: [("e", 5), ("e", 6)],
+    9: [("e", 7)],
+    10: [("e", 8)],
+    11: [("e", 9)],
+    12: [("e", 10)],
+}
+PRODUCTS = {
+    0: [("z", 0)],
+    1: [("z", 1)],
+    2: [("z", 2)],
+    3: [("z", 3)],
+    5: [("e", 0), ("e", 1)],
+    6: [("e", 2), ("e", 3)],
+    7: [("e", 4)],
+    8: [("e", 5), ("e", 6)],
+    9: [("e", 7)],
+    10: [("e", 8)],
+    11: [("e", 9)],
+}
+WIDTH = {"c": UNIT, "z": UNIT, "e": UNIT, "u": UNIT // 2}
+
+
+def tile_scaled_completion_gradient_s11_kernel(tc, u, v_words, v_scales, c, y, mask, out):
+    nc = tc.nc
+
+    with ExitStack() as ctx:
+        keep = ctx.enter_context(tc.tile_pool(name="keep", bufs=1))
+        psum = ctx.enter_context(tc.psum_pool(name="psum", bufs=1))
+        ctx.enter_context(tc.manual_schedule())
+
+        def tiles(name, count, shape, dtype):
+            return [keep.tile(shape, dtype, name="%s%d" % (name, k), align_bytes=64) for k in range(count)]
+
+        banks = [psum.tile([P, CHUNK], F32, name="bank%d" % k) for k in range(8)]
+        pred_banks, scalar_banks = banks[:4], banks[4:]
+        bank_uses = []
+
+        def scalar_bank():
+            bank_uses.append(None)
+            return scalar_banks[len(bank_uses) % len(scalar_banks)]
+
+        ident = keep.tile([P, P], F32, name="ident", align_bytes=64)
+        v_plane = keep.tile([P, N], U8, name="v_plane", align_bytes=64)
+        v_codes = tiles("v_codes", 2, [P, N], U8)
+        c_raw = keep.tile([P, 4, R], BF16, name="c_raw", align_bytes=64)
+        u_loads = [(0, 2), (2, 4), (4, 8), (8, 12)]
+        u_raw = [keep.tile([P, (b - a) * R], BF16, name="u_raw%d" % a, align_bytes=64) for a, b in u_loads]
+        y_ring = [tiles("y%d_" % k, 2, [P, N // 2], BF16) for k in range(RING_IN)]
+        mask_ring = tiles("mask", RING_IN, [P, N], BF16)
+        diff_v = tiles("diff_v", 2, [P, 2 * CHUNK], F32)
+        diff_g = tiles("diff_g", 3, [P, CHUNK], F32)
+        e_v = tiles("e_v", RING_E, [P, 2 * CHUNK], BF16)
+        e_g = [tiles("e_g%d_" % k, 2, [P, CHUNK], BF16) for k in range(RING_E)]
+        zt = tiles("zt", 8, [P, CHUNK], BF16)
+        stage = tiles("stage", RING_STAGE, [P, 2 * UNIT], BF16)
+        head_stage = tiles("head_stage", 2, [P, CHUNK], BF16)
+        tail_stage = tiles("tail_stage", 2, [P, 2 * CHUNK], BF16)
+        result = tiles("result", RING_OUT, [P, R], F32)
+
+        staged, quantised, calls = {}, {}, {}
+        for step, units in QUANTS.items():
+            width = sum(WIDTH[kind] for kind, index in units)
+            codes = keep.tile([P, width // 4], U32, name="codes%d" % step, align_bytes=64)
+            scales = keep.tile([P, width // 4], U8, name="scales%d" % step, align_bytes=64)
+            source = stage[step % RING_STAGE]
+            calls[step] = (codes[:], scales[:], source[:, 0:width])
+            at = 0
+            for unit in units:
+                w = WIDTH[unit[0]]
+                staged[unit] = source[:, at : at + w]
+                quantised[unit] = (codes[:, at // 4 : (at + w) // 4], scales[:, at // 4 : (at + w) // 4])
+                at = at + w
+
+        def own_call(name, source):
+            width = source.shape[1]
+            codes = keep.tile([P, width // 4], U32, name="codes_" + name, align_bytes=64)
+            scales = keep.tile([P, width // 4], U8, name="scales_" + name, align_bytes=64)
+            return (codes[:], scales[:], source[:])
+
+        def quantise(call):
+            codes, scales, source = call
+            nc.vector.quantize_mx(out=codes.bitcast(FP8X4), scales=scales, in_=source)
+
+        def columns(pair, start, width):
+            return (pair[0][:, start : start + width].bitcast(FP8X4), pair[1][:, start : start + width])
+
+        head_calls = [own_call("u%d" % k, head_stage[k]) for k in range(2)]
+        tail_calls = [own_call("e%d" % k, tail_stage[k]) for k in range(2)]
+
+        def u_operand(i):
+            if i < 2:
+                return columns(head_calls[i], 0, P)
+            return columns(quantised[("u", i - i % 2)], (i % 2) * P, P)
+
+        def e_operand(i, g):
+            place = CHUNK_ORDER.index(g)
+            if i == TILES - 1:
+                return columns(tail_calls[place // 2], (place % 2) * P, P)
+            return columns(quantised[("e", i)], place * P, P)
+
+        def v_operand(g):
+            codes = v_codes[g // 2][:, (g % 2) * 2 * CHUNK : (g % 2 + 1) * 2 * CHUNK]
+            return (codes.bitcast(FP4X4), v_plane[:, g * CHUNK : (g + 1) * CHUNK])
+
+        def mx(bank, stationary, moving, start=True, stop=True):
+            nc.tensor.matmul_mx(out=bank, lhsT=stationary[0], lhsT_scale=stationary[1],
+                                rhs=moving[0], rhs_scale=moving[1], start=start, stop=stop)
+
+        def turn(halves, target):
+            bank = scalar_bank()
+            for k, words in enumerate(halves):
+                nc.tensor.transpose(bank[:, k * P : (k + 1) * P], words, ident[:])
+            sets = len(halves) // 2
+            nc.scalar.copy(
+                out=target.bitcast(F32).rearrange("p (s m h) -> p s m h", s=sets, h=2),
+                in_=bank[:, 0 : sets * 2 * P].rearrange("p (s h m) -> p s m h", s=sets, h=2),
+            )
+
+        def u_halves(i):
+            k = [a <= i < b for a, b in u_loads].index(True)
+            at = (i - u_loads[k][0]) * (R // 2)
+            words = u_raw[k][:].bitcast(F32)
+            return [words[:, at + h : at + R // 2 : 2] for h in range(2)]
+
+        def sorted_halves(tile, sets):
+            words = tile[:].bitcast(F32)
+            return [words[:, (h * sets + s) * P : (h * sets + s + 1) * P] for s in range(sets) for h in range(2)]
+
+        def e_halves(i):
+            pair = e_g[i % RING_E]
+            return [sorted_halves(e_v[i % RING_E], 2), sorted_halves(pair[0], 1) + sorted_halves(pair[1], 1)]
+
+        def turn_unit(unit):
+            kind, index = unit
+            if kind == "u":
+                turn(u_halves(index) + u_halves(index + 1), staged[unit])
+                return
+            if kind == "e":
+                groups = e_halves(index)
+            else:
+                rows = [sorted_halves(zt[(index % 2) * 4 + jt], 1) for jt in range(4)]
+                groups = [rows[0] + rows[1], rows[2] + rows[3]]
+            for k, halves in enumerate(groups):
+                turn(halves, staged[unit][:, k * UNIT // 2 : (k + 1) * UNIT // 2])
+
+        def predict(i, g):
+            mx(pred_banks[g][:], u_operand(i), v_operand(g))
+
+        def z_product(g):
+            for jt in range(4):
+                bank = scalar_bank()
+                mx(bank[:], columns(quantised[("c", 0)], jt * P, P), v_operand(g))
+                nc.scalar.copy(
+                    out=zt[(g % 2) * 4 + jt][:].rearrange("p (h q r) -> p h q r", h=2, r=16),
+                    in_=bank[:].rearrange("p (q h r) -> p h q r", h=2, r=16),
+                )
+
+        def out_product(i):
+            bank = scalar_bank()
+            for k, g in enumerate(CHUNK_ORDER):
+                mx(bank[:], e_operand(i, g), columns(quantised[("z", g)], 0, R), start=(k == 0), stop=(k == CHUNKS - 1))
+            res = result[i % RING_OUT]
+            nc.scalar.copy(out=res[:], in_=bank[:])
+            nc.sync.dma_start(out=out[i * P : (i + 1) * P, :], in_=res[:])
+
+        def diff_of(i, g):
+            if g in VECTOR_CHUNKS:
+                k = VECTOR_CHUNKS.index(g)
+                return diff_v[i % 2][:, k * CHUNK : (k + 1) * CHUNK]
+            return diff_g[(2 * i + GPSIMD_CHUNKS.index(g)) % 3][:]
+
+        def subtract(i, g):
+            ratings = y_ring[i % RING_IN][g // 2][:, (g % 2) * CHUNK : (g % 2 + 1) * CHUNK]
+            nc.vector.tensor_tensor(out=diff_of(i, g), in0=pred_banks[g][:], in1=ratings, op=SUB)
+
+        def weigh(engine, target, diff, weights):
+            engine.tensor_tensor(
+                out=target.rearrange("p (h q r) -> p q h r", h=2, r=16),
+                in0=diff.rearrange("p (q h r) -> p q h r", h=2, r=16),
+                in1=weights.rearrange("p (q h r) -> p q h r", h=2, r=16),
+                op=MULT,
+            )
+
+        def weigh_single(engine, i, g):
+            weigh(engine, e_g[i % RING_E][GPSIMD_CHUNKS.index(g)][:], diff_of(i, g),
+                  mask_ring[i % RING_IN][:, g * CHUNK : (g + 1) * CHUNK])
+
+        def weigh_pair(i):
+            first = VECTOR_CHUNKS[0] * CHUNK
+            weigh(nc.vector, e_v[i % RING_E][:], diff_v[i % 2][:], mask_ring[i % RING_IN][:, first : first + 2 * CHUNK])
+
+        def load_y(i, half):
+            nc.sync.dma_start(out=y_ring[i % RING_IN][half][:],
+                              in_=y[i * P : (i + 1) * P, half * N // 2 : (half + 1) * N // 2])
+
+        def load_mask(i):
+            nc.sync.dma_start(out=mask_ring[i % RING_IN][:], in_=mask[i * P : (i + 1) * P, :])
+
+        def load_tile(i):
+            load_y(i, 0)
+            load_y(i, 1)
+            load_mask(i)
+
+        def load_u(k):
+            a, b = u_loads[k]
+            nc.sync.dma_start(out=u_raw[k][:].rearrange("p (t k) -> p t k", k=R),
+                              in_=u[a * P : b * P, :].rearrange("(t p) k -> p t k", p=P))
+
+        def load_v(half):
+            nc.sync.dma_start(out=v_codes[half][:].bitcast(I32),
+                              in_=v_words[0, :, half * N : (half + 1) * N].bitcast(I32))
+
+        nc.vector.memset(v_plane[:].bitcast(I32), 0)
+        make_identity(nc, ident[:])
+        load_u(0)
+        for r in range(4):
+            nc.sync.dma_start(out=v_plane[r:P:32, :].bitcast(I32), in_=v_scales[0, r:16:4, :].bitcast(I32))
+        nc.sync.dma_start(out=c_raw[:], in_=c.rearrange("(p t) j -> p t j", t=4))
+        load_v(0)
+        load_y(0, 0)
+        load_v(1)
+        load_y(0, 1)
+        load_mask(0)
+        load_u(1)
+        load_tile(1)
+        load_u(2)
+        load_tile(2)
+        load_tile(3)
+        load_u(3)
+        for i in range(4, RING_IN):
+            load_tile(i)
+
+        for k in range(2):
+            turn(u_halves(k), head_stage[k][:])
+        quantise(head_calls[0])
+        c_sorted = staged[("c", 0)].rearrange("p (j t) -> p j t", t=4)
+        c_source = c_raw[:].rearrange("p t j -> p j t")
+        nc.vector.tensor_copy(out=c_sorted[:, 0 : R // 2, :], in_=c_source[:, 0 : R // 2, :])
+        nc.scalar.copy(out=c_sorted[:, R // 2 : R, :], in_=c_source[:, R // 2 : R, :])
+        quantise(head_calls[1])
+        for g in (1, 0, 2, 3):
+            predict(0, g)
+
+        for i in range(TILES):
+            last = i == TILES - 1
+            subtract(i, 1)
+            subtract(i, 0)
+            for unit in TURNS.get(i, []):
+                turn_unit(unit)
+            quantise(calls[i])
+            weigh_single(nc.gpsimd, i, 0)
+            if not last:
+                predict(i + 1, 1)
+                predict(i + 1, 0)
+            for kind, index in PRODUCTS.get(i, []):
+                if kind == "z":
+                    z_product(index)
+                else:
+                    out_product(index)
+            subtract(i, 2)
+            subtract(i, 3)
+            if not last:
+                weigh_pair(i)
+                weigh_single(nc.gpsimd, i, 3)
+                predict(i + 1, 2)
+                predict(i + 1, 3)
+                if i + RING_IN < TILES:
+                    load_tile(i + RING_IN)
+
+        i = TILES - 1
+        quantise(calls[TILES])
+        out_product(i - 1)
+        weigh_pair(i)
+        groups = e_halves(i)
+        turn(groups[0], tail_stage[0][:])
+        weigh_single(nc.vector, i, 3)
+        turn(groups[1], tail_stage[1][:])
+        quantise(tail_calls[0])
+        quantise(tail_calls[1])
+        out_product(i)

@@ -20,59 +20,27 @@ P = 128
 CHUNK = 512
 TILES = M // P
 CHUNKS = N // CHUNK
-UNIT = 2048
+BLOCK = 32
+RUN = 16
 
-VECTOR_CHUNKS = (1, 2)
-GPSIMD_CHUNKS = (0, 3)
-CHUNK_ORDER = VECTOR_CHUNKS + GPSIMD_CHUNKS
+GPSIMD_COLUMNS = 832
+GATE_COLUMNS = 64
 
 RING_IN = 8
 RING_E = 5
 RING_OUT = 4
-RING_STAGE = 3
+RING_STAGE = 7
 
-TURNS = {
-    1: [("u", 2), ("z", 0)],
-    2: [("u", 4), ("u", 6), ("z", 1)],
-    3: [("z", 2), ("e", 0)],
-    4: [("z", 3), ("e", 1), ("e", 2), ("e", 3)],
-    5: [("e", 4), ("u", 8)],
-    6: [("e", 5), ("u", 10)],
-    7: [("e", 6)],
-    8: [("e", 7)],
-    9: [("e", 8)],
-    10: [("e", 9)],
-    11: [("e", 10)],
-}
-QUANTS = {
-    0: [("c", 0)],
-    1: [("u", 2)],
-    2: [("z", 0)],
-    3: [("z", 1), ("u", 4), ("u", 6)],
-    4: [("z", 2), ("e", 0)],
-    5: [("z", 3), ("e", 1)],
-    6: [("e", 2), ("e", 3)],
-    7: [("e", 4), ("u", 8), ("u", 10)],
-    8: [("e", 5), ("e", 6)],
-    9: [("e", 7)],
-    10: [("e", 8)],
-    11: [("e", 9)],
-    12: [("e", 10)],
-}
-PRODUCTS = {
-    0: [("z", 0)],
-    1: [("z", 1)],
-    2: [("z", 2)],
-    3: [("z", 3)],
-    5: [("e", 0), ("e", 1)],
-    6: [("e", 2), ("e", 3)],
-    7: [("e", 4)],
-    8: [("e", 5), ("e", 6)],
-    9: [("e", 7)],
-    10: [("e", 8)],
-    11: [("e", 9)],
-}
-WIDTH = {"c": UNIT, "z": UNIT, "e": UNIT, "u": UNIT // 2}
+E_TURNS = {}
+E_QUANTS = {}
+OUTS = {}
+Z_TURNS = {}
+Z_QUANTS = {}
+Z_PRODUCTS = {}
+QUANTS = {0: [("qc", 0), ("qu", 2)], 1: [("qu", 3)], 2: [("qz", 0), ("qz", 1), ("qu", 4)], 3: [("qz", 2), ("qu", 5)], 4: [("qe", 0), ("qz", 3), ("qu", 6)], 5: [("qe", 1), ("qe", 2), ("qu", 7)], 6: [("qe", 3), ("qe", 4), ("qu", 8)], 7: [("qe", 5), ("qu", 9)], 8: [("qe", 6), ("qu", 10)], 9: [("qe", 7), ("qu", 11)], 10: [("qe", 8)]}
+MID = {0: [("z", 0)], 1: [("tz", 0), ("tu", 4)], 2: [("tz", 2), ("tu", 5)], 3: [("tz", 3), ("tu", 6), ("te", 0)], 4: [("tu", 7), ("te", 1), ("te", 2)], 5: [("tu", 8), ("te", 3), ("te", 4), ("o", 1)], 6: [("tu", 9), ("te", 5), ("o", 3)], 7: [("tu", 10), ("te", 6), ("o", 5)], 8: [("tu", 11), ("te", 7), ("o", 6)], 9: [("te", 8), ("o", 7)], 10: [("te", 9), ("o", 8)]}
+LATE = {0: [("z", 1)], 1: [("tz", 1), ("z", 2)], 2: [("z", 3)], 4: [("o", 0)], 5: [("o", 2)], 6: [("o", 4)]}
+LATEQ = {10: [("qe", 9)]}
 
 
 def tile_scaled_completion_gradient_s11_kernel(tc, u, v_words, v_scales, c, y, mask, out):
@@ -98,60 +66,39 @@ def tile_scaled_completion_gradient_s11_kernel(tc, u, v_words, v_scales, c, y, m
         v_plane = keep.tile([P, N], U8, name="v_plane", align_bytes=64)
         v_codes = tiles("v_codes", 2, [P, N], U8)
         c_raw = keep.tile([P, 4, R], BF16, name="c_raw", align_bytes=64)
-        u_loads = [(0, 2), (2, 4), (4, 8), (8, 12)]
+        u_loads = [(0, 1), (1, 2), (2, 4), (4, 8), (8, 12)]
         u_raw = [keep.tile([P, (b - a) * R], BF16, name="u_raw%d" % a, align_bytes=64) for a, b in u_loads]
-        y_ring = [tiles("y%d_" % k, 2, [P, N // 2], BF16) for k in range(RING_IN)]
+        y_ring = tiles("y", RING_IN, [P, N], BF16)
         mask_ring = tiles("mask", RING_IN, [P, N], BF16)
-        diff_v = tiles("diff_v", 2, [P, 2 * CHUNK], F32)
-        diff_g = tiles("diff_g", 3, [P, CHUNK], F32)
-        e_v = tiles("e_v", RING_E, [P, 2 * CHUNK], BF16)
-        e_g = [tiles("e_g%d_" % k, 2, [P, CHUNK], BF16) for k in range(RING_E)]
-        zt = tiles("zt", 8, [P, CHUNK], BF16)
-        stage = tiles("stage", RING_STAGE, [P, 2 * UNIT], BF16)
-        head_stage = tiles("head_stage", 2, [P, CHUNK], BF16)
-        tail_stage = tiles("tail_stage", 2, [P, 2 * CHUNK], BF16)
+        diff = tiles("diff", 2, [P, N], F32)
+        e_sorted = [tiles("e_sorted%d_" % k, 2, [P, N // 2], BF16) for k in range(RING_E)]
+        z_sorted = tiles("z_sorted", 8, [P, CHUNK], BF16)
+        stage = tiles("stage", RING_STAGE, [P, N], BF16)
+        u_stage = tiles("u_stage", 4, [P, R], BF16)
         result = tiles("result", RING_OUT, [P, R], F32)
 
-        staged, quantised, calls = {}, {}, {}
-        for step, units in QUANTS.items():
-            width = sum(WIDTH[kind] for kind, index in units)
-            codes = keep.tile([P, width // 4], U32, name="codes%d" % step, align_bytes=64)
-            scales = keep.tile([P, width // 4], U8, name="scales%d" % step, align_bytes=64)
-            source = stage[step % RING_STAGE]
-            calls[step] = (codes[:], scales[:], source[:, 0:width])
-            at = 0
-            for unit in units:
-                w = WIDTH[unit[0]]
-                staged[unit] = source[:, at : at + w]
-                quantised[unit] = (codes[:, at // 4 : (at + w) // 4], scales[:, at // 4 : (at + w) // 4])
-                at = at + w
+        def operand_tiles(name, count, width):
+            return list(zip(tiles(name + "_codes", count, [P, width], U32), tiles(name + "_scales", count, [P, width], U8)))
 
-        def own_call(name, source):
-            width = source.shape[1]
-            codes = keep.tile([P, width // 4], U32, name="codes_" + name, align_bytes=64)
-            scales = keep.tile([P, width // 4], U8, name="scales_" + name, align_bytes=64)
-            return (codes[:], scales[:], source[:])
+        u_mx = operand_tiles("u", TILES, P)
+        c_mx = operand_tiles("c", 1, R)
+        z_mx = operand_tiles("z", CHUNKS, R)
+        e_mx = operand_tiles("e", 6, CHUNKS * P)
 
-        def quantise(call):
-            codes, scales, source = call
-            nc.vector.quantize_mx(out=codes.bitcast(FP8X4), scales=scales, in_=source)
+        staged = {}
+
+        def stage_of(unit):
+            if unit not in staged:
+                staged[unit] = stage[len(staged) % RING_STAGE]
+            return staged[unit]
+
+        def quantise(pair, source, start=0):
+            words = source.shape[1] // 4
+            nc.vector.quantize_mx(out=pair[0][:, start : start + words].bitcast(FP8X4),
+                                  scales=pair[1][:, start : start + words], in_=source)
 
         def columns(pair, start, width):
             return (pair[0][:, start : start + width].bitcast(FP8X4), pair[1][:, start : start + width])
-
-        head_calls = [own_call("u%d" % k, head_stage[k]) for k in range(2)]
-        tail_calls = [own_call("e%d" % k, tail_stage[k]) for k in range(2)]
-
-        def u_operand(i):
-            if i < 2:
-                return columns(head_calls[i], 0, P)
-            return columns(quantised[("u", i - i % 2)], (i % 2) * P, P)
-
-        def e_operand(i, g):
-            place = CHUNK_ORDER.index(g)
-            if i == TILES - 1:
-                return columns(tail_calls[place // 2], (place % 2) * P, P)
-            return columns(quantised[("e", i)], place * P, P)
 
         def v_operand(g):
             codes = v_codes[g // 2][:, (g % 2) * 2 * CHUNK : (g % 2 + 1) * 2 * CHUNK]
@@ -171,89 +118,82 @@ def tile_scaled_completion_gradient_s11_kernel(tc, u, v_words, v_scales, c, y, m
                 in_=bank[:, 0 : sets * 2 * P].rearrange("p (s h m) -> p s m h", s=sets, h=2),
             )
 
-        def u_halves(i):
+        def turn_u(i):
             k = [a <= i < b for a, b in u_loads].index(True)
             at = (i - u_loads[k][0]) * (R // 2)
             words = u_raw[k][:].bitcast(F32)
-            return [words[:, at + h : at + R // 2 : 2] for h in range(2)]
+            turn([words[:, at + h : at + R // 2 : 2] for h in range(2)], u_stage[i % 4][:])
 
-        def sorted_halves(tile, sets):
+        def sorted_halves(tile, sets, s):
             words = tile[:].bitcast(F32)
-            return [words[:, (h * sets + s) * P : (h * sets + s + 1) * P] for s in range(sets) for h in range(2)]
+            return [words[:, (h * sets + s) * P : (h * sets + s + 1) * P] for h in range(2)]
 
-        def e_halves(i):
-            pair = e_g[i % RING_E]
-            return [sorted_halves(e_v[i % RING_E], 2), sorted_halves(pair[0], 1) + sorted_halves(pair[1], 1)]
+        def e_tile(i, g):
+            if i == TILES - 1 and g == CHUNKS - 1:
+                return e_sorted[(i + 1) % RING_E][1]
+            return e_sorted[i % RING_E][g // 2]
 
-        def turn_unit(unit):
-            kind, index = unit
-            if kind == "u":
-                turn(u_halves(index) + u_halves(index + 1), staged[unit])
-                return
-            if kind == "e":
-                groups = e_halves(index)
-            else:
-                rows = [sorted_halves(zt[(index % 2) * 4 + jt], 1) for jt in range(4)]
-                groups = [rows[0] + rows[1], rows[2] + rows[3]]
-            for k, halves in enumerate(groups):
-                turn(halves, staged[unit][:, k * UNIT // 2 : (k + 1) * UNIT // 2])
+        def turn_e(i, first, count):
+            halves = [w for g in range(first, first + count) for w in sorted_halves(e_tile(i, g), 2, g % 2)]
+            turn(halves, stage_of(("e", i))[:, first * CHUNK : (first + count) * CHUNK])
+
+        def turn_z(g):
+            for first in (0, 2):
+                halves = [w for jt in (first, first + 1) for w in sorted_halves(z_sorted[(g % 2) * 4 + jt], 1, 0)]
+                turn(halves, stage_of(("z", g))[:, first * CHUNK : (first + 2) * CHUNK])
 
         def predict(i, g):
-            mx(pred_banks[g][:], u_operand(i), v_operand(g))
+            mx(pred_banks[g][:], columns(u_mx[i], 0, P), v_operand(g))
 
         def z_product(g):
             for jt in range(4):
                 bank = scalar_bank()
-                mx(bank[:], columns(quantised[("c", 0)], jt * P, P), v_operand(g))
+                mx(bank[:], columns(c_mx[0], jt * P, P), v_operand(g))
                 nc.scalar.copy(
-                    out=zt[(g % 2) * 4 + jt][:].rearrange("p (h q r) -> p h q r", h=2, r=16),
-                    in_=bank[:].rearrange("p (q h r) -> p h q r", h=2, r=16),
+                    out=z_sorted[(g % 2) * 4 + jt][:].rearrange("p (h q r) -> p h q r", h=2, r=RUN),
+                    in_=bank[:].rearrange("p (q h r) -> p h q r", h=2, r=RUN),
                 )
 
-        def out_product(i):
-            bank = scalar_bank()
-            for k, g in enumerate(CHUNK_ORDER):
-                mx(bank[:], e_operand(i, g), columns(quantised[("z", g)], 0, R), start=(k == 0), stop=(k == CHUNKS - 1))
+        out_banks = {}
+
+        def out_product(i, first=0, count=CHUNKS):
+            if first == 0:
+                out_banks[i] = scalar_bank()
+            bank = out_banks[i]
+            for g in range(first, first + count):
+                mx(bank[:], columns(e_mx[i % 6], g * P, P), columns(z_mx[g], 0, R), start=(g == 0), stop=(g == CHUNKS - 1))
+            if first + count < CHUNKS:
+                return
             res = result[i % RING_OUT]
             nc.scalar.copy(out=res[:], in_=bank[:])
             nc.sync.dma_start(out=out[i * P : (i + 1) * P, :], in_=res[:])
 
-        def diff_of(i, g):
-            if g in VECTOR_CHUNKS:
-                k = VECTOR_CHUNKS.index(g)
-                return diff_v[i % 2][:, k * CHUNK : (k + 1) * CHUNK]
-            return diff_g[(2 * i + GPSIMD_CHUNKS.index(g)) % 3][:]
+        def subtract(i, lo, hi):
+            g = lo // CHUNK
+            nc.vector.tensor_tensor(out=diff[i % 2][:, lo:hi], in0=pred_banks[g][:, lo - g * CHUNK : hi - g * CHUNK],
+                                    in1=y_ring[i % RING_IN][:, lo:hi], op=SUB)
 
-        def subtract(i, g):
-            ratings = y_ring[i % RING_IN][g // 2][:, (g % 2) * CHUNK : (g % 2 + 1) * CHUNK]
-            nc.vector.tensor_tensor(out=diff_of(i, g), in0=pred_banks[g][:], in1=ratings, op=SUB)
-
-        def weigh(engine, target, diff, weights):
+        def weigh(engine, i, lo, hi):
+            target = e_tile(i, lo // CHUNK)[:].rearrange("p (h q r) -> p q h r", h=2, r=RUN)
+            base = lo - lo % (N // 2)
             engine.tensor_tensor(
-                out=target.rearrange("p (h q r) -> p q h r", h=2, r=16),
-                in0=diff.rearrange("p (q h r) -> p q h r", h=2, r=16),
-                in1=weights.rearrange("p (q h r) -> p q h r", h=2, r=16),
+                out=target[:, (lo - base) // BLOCK : (hi - base) // BLOCK, :, :],
+                in0=diff[i % 2][:, lo:hi].rearrange("p (q h r) -> p q h r", h=2, r=RUN),
+                in1=mask_ring[i % RING_IN][:, lo:hi].rearrange("p (q h r) -> p q h r", h=2, r=RUN),
                 op=MULT,
             )
 
-        def weigh_single(engine, i, g):
-            weigh(engine, e_g[i % RING_E][GPSIMD_CHUNKS.index(g)][:], diff_of(i, g),
-                  mask_ring[i % RING_IN][:, g * CHUNK : (g + 1) * CHUNK])
+        def quantise_e(i, first=0, count=CHUNKS):
+            quantise(e_mx[i % 6], stage_of(("e", i))[:, first * CHUNK : (first + count) * CHUNK], first * P)
 
-        def weigh_pair(i):
-            first = VECTOR_CHUNKS[0] * CHUNK
-            weigh(nc.vector, e_v[i % RING_E][:], diff_v[i % 2][:], mask_ring[i % RING_IN][:, first : first + 2 * CHUNK])
-
-        def load_y(i, half):
-            nc.sync.dma_start(out=y_ring[i % RING_IN][half][:],
-                              in_=y[i * P : (i + 1) * P, half * N // 2 : (half + 1) * N // 2])
+        def load_y(i, lo, hi):
+            nc.sync.dma_start(out=y_ring[i % RING_IN][:, lo:hi], in_=y[i * P : (i + 1) * P, lo:hi])
 
         def load_mask(i):
             nc.sync.dma_start(out=mask_ring[i % RING_IN][:], in_=mask[i * P : (i + 1) * P, :])
 
         def load_tile(i):
-            load_y(i, 0)
-            load_y(i, 1)
+            load_y(i, 0, N)
             load_mask(i)
 
         def load_u(k):
@@ -265,71 +205,114 @@ def tile_scaled_completion_gradient_s11_kernel(tc, u, v_words, v_scales, c, y, m
             nc.sync.dma_start(out=v_codes[half][:].bitcast(I32),
                               in_=v_words[0, :, half * N : (half + 1) * N].bitcast(I32))
 
+        def load_c():
+            nc.sync.dma_start(out=c_raw[:], in_=c.rearrange("(p t) j -> p t j", t=4))
+
         nc.vector.memset(v_plane[:].bitcast(I32), 0)
         make_identity(nc, ident[:])
         load_u(0)
         for r in range(4):
             nc.sync.dma_start(out=v_plane[r:P:32, :].bitcast(I32), in_=v_scales[0, r:16:4, :].bitcast(I32))
-        nc.sync.dma_start(out=c_raw[:], in_=c.rearrange("(p t) j -> p t j", t=4))
         load_v(0)
-        load_y(0, 0)
-        load_v(1)
-        load_y(0, 1)
-        load_mask(0)
+        load_y(0, 0, N // 2)
         load_u(1)
-        load_tile(1)
+        load_c()
+        load_v(1)
+        load_y(0, N // 2, N)
         load_u(2)
+        load_mask(0)
+        load_y(1, 0, N)
+        load_mask(1)
+        load_u(3)
         load_tile(2)
         load_tile(3)
-        load_u(3)
+        load_u(4)
         for i in range(4, RING_IN):
             load_tile(i)
 
-        for k in range(2):
-            turn(u_halves(k), head_stage[k][:])
-        quantise(head_calls[0])
-        c_sorted = staged[("c", 0)].rearrange("p (j t) -> p j t", t=4)
+        c_sorted = stage_of(("c", 0))[:].rearrange("p (j t) -> p j t", t=4)
         c_source = c_raw[:].rearrange("p t j -> p j t")
-        nc.vector.tensor_copy(out=c_sorted[:, 0 : R // 2, :], in_=c_source[:, 0 : R // 2, :])
-        nc.scalar.copy(out=c_sorted[:, R // 2 : R, :], in_=c_source[:, R // 2 : R, :])
-        quantise(head_calls[1])
-        for g in (1, 0, 2, 3):
-            predict(0, g)
+        turn_u(0)
+        quantise(u_mx[0], u_stage[0][:])
+        def job(kind, k):
+            if kind == "tu":
+                turn_u(k)
+            elif kind == "tz":
+                turn_z(k)
+            elif kind == "te":
+                turn_e(k, 0, 2)
+                turn_e(k, 2, 2)
+            elif kind == "z":
+                z_product(k)
+            elif kind == "o":
+                out_product(k)
+            elif kind == "qu":
+                quantise(u_mx[k], u_stage[k % 4][:])
+            elif kind == "qc":
+                quantise(c_mx[0], stage_of(("c", 0))[:])
+            elif kind == "qz":
+                quantise(z_mx[k], stage_of(("z", k))[:])
+            elif kind == "qe":
+                quantise_e(k)
+            elif kind == "cv":
+                nc.vector.tensor_copy(out=c_sorted[:, 0 : R // 2, :], in_=c_source[:, 0 : R // 2, :])
 
-        for i in range(TILES):
-            last = i == TILES - 1
-            subtract(i, 1)
-            subtract(i, 0)
-            for unit in TURNS.get(i, []):
-                turn_unit(unit)
-            quantise(calls[i])
-            weigh_single(nc.gpsimd, i, 0)
-            if not last:
-                predict(i + 1, 1)
-                predict(i + 1, 0)
-            for kind, index in PRODUCTS.get(i, []):
-                if kind == "z":
-                    z_product(index)
-                else:
-                    out_product(index)
-            subtract(i, 2)
-            subtract(i, 3)
-            if not last:
-                weigh_pair(i)
-                weigh_single(nc.gpsimd, i, 3)
-                predict(i + 1, 2)
-                predict(i + 1, 3)
-                if i + RING_IN < TILES:
-                    load_tile(i + RING_IN)
+        predict(0, 0)
+        predict(0, 1)
+        turn_u(1)
+        predict(0, 2)
+        predict(0, 3)
+        nc.scalar.copy(out=c_sorted[:, R // 2 : R, :], in_=c_source[:, R // 2 : R, :])
+        turn_u(2)
+        turn_u(3)
+
+        split = N - GPSIMD_COLUMNS
+        gate = N - GATE_COLUMNS
+        for i in range(TILES - 1):
+            for g in range(CHUNKS):
+                subtract(i, g * CHUNK, min((g + 1) * CHUNK, gate))
+                if i == 0 and g == 1:
+                    job("cv", 0)
+                    job("qu", 1)
+                    predict(1, 0)
+                if g < CHUNKS - 1 and (i, g) != (0, 0):
+                    predict(i + 1, g)
+            for kind, k in QUANTS.get(i, []) + MID.get(i, []):
+                job(kind, k)
+            if split > N // 2:
+                weigh(nc.vector, i, N // 2, split)
+            if i < TILES - 2 and i not in LATEQ:
+                subtract(i, gate, N)
+                weigh(nc.vector, i, 0, N // 2)
+            else:
+                weigh(nc.vector, i, 0, N // 2)
+                for kind, k in LATEQ.get(i, []):
+                    job(kind, k)
+                subtract(i, gate, N)
+            weigh(nc.gpsimd, i, split, N)
+            predict(i + 1, CHUNKS - 1)
+            for kind, k in LATE.get(i, []):
+                job(kind, k)
+            if i + RING_IN < TILES:
+                load_tile(i + RING_IN)
 
         i = TILES - 1
-        quantise(calls[TILES])
-        out_product(i - 1)
-        weigh_pair(i)
-        groups = e_halves(i)
-        turn(groups[0], tail_stage[0][:])
-        weigh_single(nc.vector, i, 3)
-        turn(groups[1], tail_stage[1][:])
-        quantise(tail_calls[0])
-        quantise(tail_calls[1])
+        turn_e(i - 1, 0, 2)
+        out_product(i - 2)
+        for g in range(CHUNKS):
+            subtract(i, g * CHUNK, (g + 1) * CHUNK)
+        turn_e(i - 1, 2, 2)
+        quantise_e(i - 1, 0, 2)
+        out_product(i - 1, 0, 2)
+        weigh(nc.vector, i, 0, 2 * CHUNK)
+        turn_e(i, 0, 2)
+        quantise_e(i - 1, 2, 2)
+        out_product(i - 1, 2, 2)
+        weigh(nc.vector, i, 2 * CHUNK, 3 * CHUNK)
+        turn_e(i, 2, 1)
+        weigh(nc.vector, i, 3 * CHUNK, N)
+        turn_e(i, 3, 1)
+        quantise_e(i, 0, 2)
+        quantise_e(i, 2, 1)
+        quantise_e(i, 3, 1)
         out_product(i)

@@ -13,34 +13,32 @@ U32 = mybir.dt.uint32
 U8 = mybir.dt.uint8
 FP8X4 = mybir.dt.float8_e4m3fn_x4
 FP4X4 = mybir.dt.float4_e2m1fn_x4
-SUB = mybir.AluOpType.subtract
-MULT = mybir.AluOpType.mult
 
 P = 128
+PACK = 4
 CHUNK = 512
 TILES = M // P
 CHUNKS = N // CHUNK
-BLOCK = 32
+HALF = N // 2
 RUN = 16
+LAST = TILES - 1
 
-GPSIMD_COLUMNS = 832
-GATE_COLUMNS = 64
+GATE = 64
+U_GROUPS = [(0, 1), (1, 2), (2, 4), (4, 8), (8, 12)]
+U_LOADS = [(0, 2), (2, 4), (4, 8), (8, 12)]
+C_VECTOR = 320
+U_TURNS = {1: 3, 5: 4}
+Z_DONE = CHUNKS
 
 RING_IN = 8
-RING_E = 5
+RING_E = 4
 RING_OUT = 4
-RING_STAGE = 7
+RING_STAGE = 5
+WIDEST = 2 * N
 
-E_TURNS = {}
-E_QUANTS = {}
-OUTS = {}
-Z_TURNS = {}
-Z_QUANTS = {}
-Z_PRODUCTS = {}
-QUANTS = {0: [("qc", 0), ("qu", 2)], 1: [("qu", 3)], 2: [("qz", 0), ("qz", 1), ("qu", 4)], 3: [("qz", 2), ("qu", 5)], 4: [("qe", 0), ("qz", 3), ("qu", 6)], 5: [("qe", 1), ("qe", 2), ("qu", 7)], 6: [("qe", 3), ("qe", 4), ("qu", 8)], 7: [("qe", 5), ("qu", 9)], 8: [("qe", 6), ("qu", 10)], 9: [("qe", 7), ("qu", 11)], 10: [("qe", 8)]}
-MID = {0: [("z", 0)], 1: [("tz", 0), ("tu", 4)], 2: [("tz", 2), ("tu", 5)], 3: [("tz", 3), ("tu", 6), ("te", 0)], 4: [("tu", 7), ("te", 1), ("te", 2)], 5: [("tu", 8), ("te", 3), ("te", 4), ("o", 1)], 6: [("tu", 9), ("te", 5), ("o", 3)], 7: [("tu", 10), ("te", 6), ("o", 5)], 8: [("tu", 11), ("te", 7), ("o", 6)], 9: [("te", 8), ("o", 7)], 10: [("te", 9), ("o", 8)]}
-LATE = {0: [("z", 1)], 1: [("tz", 1), ("z", 2)], 2: [("z", 3)], 4: [("o", 0)], 5: [("o", 2)], 6: [("o", 4)]}
-LATEQ = {10: [("qe", 9)]}
+
+def e_step(k):
+    return max(k + 2, Z_DONE + (k + 1) // 2)
 
 
 def tile_scaled_completion_gradient_s11_kernel(tc, u, v_words, v_scales, c, y, mask, out):
@@ -55,61 +53,81 @@ def tile_scaled_completion_gradient_s11_kernel(tc, u, v_words, v_scales, c, y, m
             return [keep.tile(shape, dtype, name="%s%d" % (name, k), align_bytes=64) for k in range(count)]
 
         banks = [psum.tile([P, CHUNK], F32, name="bank%d" % k) for k in range(8)]
-        pred_banks, scalar_banks = banks[:4], banks[4:]
-        bank_uses = []
+        pred_banks, scalar_banks = banks[:CHUNKS], banks[CHUNKS:]
+        scalar_bank_uses = []
 
-        def scalar_bank():
-            bank_uses.append(None)
-            return scalar_banks[len(bank_uses) % len(scalar_banks)]
+        def next_scalar_bank():
+            scalar_bank_uses.append(None)
+            return scalar_banks[len(scalar_bank_uses) % len(scalar_banks)]
 
         ident = keep.tile([P, P], F32, name="ident", align_bytes=64)
         v_plane = keep.tile([P, N], U8, name="v_plane", align_bytes=64)
         v_codes = tiles("v_codes", 2, [P, N], U8)
-        c_raw = keep.tile([P, 4, R], BF16, name="c_raw", align_bytes=64)
-        u_loads = [(0, 1), (1, 2), (2, 4), (4, 8), (8, 12)]
-        u_raw = [keep.tile([P, (b - a) * R], BF16, name="u_raw%d" % a, align_bytes=64) for a, b in u_loads]
+        c_raw = keep.tile([P, PACK, R], BF16, name="c_raw", align_bytes=64)
+        u_raw = [keep.tile([P, (b - a) * R], BF16, name="u_raw%d" % a, align_bytes=64) for a, b in U_LOADS]
         y_ring = tiles("y", RING_IN, [P, N], BF16)
         mask_ring = tiles("mask", RING_IN, [P, N], BF16)
         diff = tiles("diff", 2, [P, N], F32)
-        e_sorted = [tiles("e_sorted%d_" % k, 2, [P, N // 2], BF16) for k in range(RING_E)]
-        z_sorted = tiles("z_sorted", 8, [P, CHUNK], BF16)
-        stage = tiles("stage", RING_STAGE, [P, N], BF16)
-        u_stage = tiles("u_stage", 4, [P, R], BF16)
+        e_sorted = [tiles("e_sorted%d_" % k, 2, [P, HALF], BF16) for k in range(RING_E)]
+        z_sorted = tiles("z_sorted", 2 * PACK, [P, CHUNK], BF16)
+        stage = tiles("stage", RING_STAGE, [P, WIDEST], BF16)
         result = tiles("result", RING_OUT, [P, R], F32)
 
-        def operand_tiles(name, count, width):
-            return list(zip(tiles(name + "_codes", count, [P, width], U32), tiles(name + "_scales", count, [P, width], U8)))
+        def width_of(operand):
+            kind, k = operand
+            return (U_GROUPS[k][1] - U_GROUPS[k][0]) * R if kind == "u" else N
 
-        u_mx = operand_tiles("u", TILES, P)
-        c_mx = operand_tiles("c", 1, R)
-        z_mx = operand_tiles("z", CHUNKS, R)
-        e_mx = operand_tiles("e", 6, CHUNKS * P)
+        calls_of = {"head": [[("u", 0)], [("u", 1)], [("c", 0)]], 0: [[("u", 2)]],
+                    1: [[("z", 0)]], 2: [[("u", 3)]], 3: [[("z", 1), ("z", 2)]]}
+        for step in range(Z_DONE, LAST):
+            calls_of[step] = [[("z", CHUNKS - 1)] * (step == Z_DONE) + [("e", k) for k in range(TILES) if e_step(k) == step]]
+        calls_of[6].append([("u", 4)])
+        calls_of["tail"] = [[("e", k)] for k in range(LAST - 2, TILES)]
 
-        staged = {}
+        staged, codes_of, scales_of, whole_call = {}, {}, {}, {}
+        order = ["head"] + [step for step in range(LAST) if step in calls_of] + ["tail"]
+        for number, call in enumerate([call for step in order for call in calls_of[step]]):
+            width = sum(width_of(operand) for operand in call)
+            codes = keep.tile([P, width // PACK], U32, name="codes%d" % number, align_bytes=64)
+            scales = keep.tile([P, width // PACK], U8, name="scales%d" % number, align_bytes=64)
+            source = stage[number % RING_STAGE]
+            whole_call[call[0]] = (codes[:], scales[:], source[:, 0:width])
+            at = 0
+            for operand in call:
+                end = at + width_of(operand)
+                staged[operand] = source[:, at:end]
+                codes_of[operand] = codes[:, at // PACK : end // PACK]
+                scales_of[operand] = scales[:, at // PACK : end // PACK]
+                at = end
 
-        def stage_of(unit):
-            if unit not in staged:
-                staged[unit] = stage[len(staged) % RING_STAGE]
-            return staged[unit]
+        def quantise(codes, scales, source):
+            nc.vector.quantize_mx(out=codes.bitcast(FP8X4), scales=scales, in_=source)
 
-        def quantise(pair, source, start=0):
-            words = source.shape[1] // 4
-            nc.vector.quantize_mx(out=pair[0][:, start : start + words].bitcast(FP8X4),
-                                  scales=pair[1][:, start : start + words], in_=source)
+        def quantise_call(call):
+            quantise(*whole_call[call[0]])
 
-        def columns(pair, start, width):
-            return (pair[0][:, start : start + width].bitcast(FP8X4), pair[1][:, start : start + width])
+        def quantise_e(k, first, count):
+            words = slice(first * P, (first + count) * P)
+            quantise(codes_of[("e", k)][:, words], scales_of[("e", k)][:, words],
+                     staged[("e", k)][:, first * CHUNK : (first + count) * CHUNK])
 
-        def v_operand(g):
+        def columns(operand, start, width):
+            return (codes_of[operand][:, start : start + width].bitcast(FP8X4), scales_of[operand][:, start : start + width])
+
+        def u_columns(i):
+            k = [a <= i < b for a, b in U_GROUPS].index(True)
+            return columns(("u", k), (i - U_GROUPS[k][0]) * P, P)
+
+        def v_columns(g):
             codes = v_codes[g // 2][:, (g % 2) * 2 * CHUNK : (g % 2 + 1) * 2 * CHUNK]
             return (codes.bitcast(FP4X4), v_plane[:, g * CHUNK : (g + 1) * CHUNK])
 
-        def mx(bank, stationary, moving, start=True, stop=True):
-            nc.tensor.matmul_mx(out=bank, lhsT=stationary[0], lhsT_scale=stationary[1],
+        def mx(target, stationary, moving, start=True, stop=True):
+            nc.tensor.matmul_mx(out=target, lhsT=stationary[0], lhsT_scale=stationary[1],
                                 rhs=moving[0], rhs_scale=moving[1], start=start, stop=stop)
 
         def turn(halves, target):
-            bank = scalar_bank()
+            bank = next_scalar_bank()
             for k, words in enumerate(halves):
                 nc.tensor.transpose(bank[:, k * P : (k + 1) * P], words, ident[:])
             sets = len(halves) // 2
@@ -118,73 +136,74 @@ def tile_scaled_completion_gradient_s11_kernel(tc, u, v_words, v_scales, c, y, m
                 in_=bank[:, 0 : sets * 2 * P].rearrange("p (s h m) -> p s m h", s=sets, h=2),
             )
 
-        def turn_u(i):
-            k = [a <= i < b for a, b in u_loads].index(True)
-            at = (i - u_loads[k][0]) * (R // 2)
-            words = u_raw[k][:].bitcast(F32)
-            turn([words[:, at + h : at + R // 2 : 2] for h in range(2)], u_stage[i % 4][:])
+        def turn_u(k):
+            a, b = U_GROUPS[k]
+            load = [lo <= a < hi for lo, hi in U_LOADS].index(True)
+            words = u_raw[load][:].bitcast(F32)
+            for first in range(a, b, 2):
+                sets = [s - U_LOADS[load][0] for s in range(first, min(first + 2, b))]
+                halves = [words[:, s * R // 2 + h : (s + 1) * R // 2 : 2] for s in sets for h in range(2)]
+                turn(halves, staged[("u", k)][:, (first - a) * R : (first - a + len(sets)) * R])
 
         def sorted_halves(tile, sets, s):
             words = tile[:].bitcast(F32)
             return [words[:, (h * sets + s) * P : (h * sets + s + 1) * P] for h in range(2)]
 
         def e_tile(i, g):
-            if i == TILES - 1 and g == CHUNKS - 1:
+            if i == LAST and g == CHUNKS - 1:
                 return e_sorted[(i + 1) % RING_E][1]
             return e_sorted[i % RING_E][g // 2]
 
         def turn_e(i, first, count):
             halves = [w for g in range(first, first + count) for w in sorted_halves(e_tile(i, g), 2, g % 2)]
-            turn(halves, stage_of(("e", i))[:, first * CHUNK : (first + count) * CHUNK])
+            turn(halves, staged[("e", i)][:, first * CHUNK : (first + count) * CHUNK])
 
         def turn_z(g):
             for first in (0, 2):
-                halves = [w for jt in (first, first + 1) for w in sorted_halves(z_sorted[(g % 2) * 4 + jt], 1, 0)]
-                turn(halves, stage_of(("z", g))[:, first * CHUNK : (first + 2) * CHUNK])
+                halves = [w for j in (first, first + 1) for w in sorted_halves(z_sorted[(g % 2) * PACK + j], 1, 0)]
+                turn(halves, staged[("z", g)][:, first * CHUNK : (first + 2) * CHUNK])
 
         def predict(i, g):
-            mx(pred_banks[g][:], columns(u_mx[i], 0, P), v_operand(g))
+            mx(pred_banks[g][:], u_columns(i), v_columns(g))
 
         def z_product(g):
-            for jt in range(4):
-                bank = scalar_bank()
-                mx(bank[:], columns(c_mx[0], jt * P, P), v_operand(g))
+            for j in range(R // P):
+                bank = next_scalar_bank()
+                mx(bank[:], columns(("c", 0), j * P, P), v_columns(g))
                 nc.scalar.copy(
-                    out=z_sorted[(g % 2) * 4 + jt][:].rearrange("p (h q r) -> p h q r", h=2, r=RUN),
+                    out=z_sorted[(g % 2) * PACK + j][:].rearrange("p (h q r) -> p h q r", h=2, r=RUN),
                     in_=bank[:].rearrange("p (q h r) -> p h q r", h=2, r=RUN),
                 )
 
-        out_banks = {}
-
-        def out_product(i, first=0, count=CHUNKS):
-            if first == 0:
-                out_banks[i] = scalar_bank()
-            bank = out_banks[i]
+        def out_passes(bank, i, first, count, lo=0, hi=R):
             for g in range(first, first + count):
-                mx(bank[:], columns(e_mx[i % 6], g * P, P), columns(z_mx[g], 0, R), start=(g == 0), stop=(g == CHUNKS - 1))
-            if first + count < CHUNKS:
-                return
+                mx(bank[:, 0 : hi - lo], columns(("e", i), g * P, P), columns(("z", g), lo, hi - lo),
+                   start=(g == 0), stop=(g == CHUNKS - 1))
+
+        def store(bank, i):
             res = result[i % RING_OUT]
             nc.scalar.copy(out=res[:], in_=bank[:])
             nc.sync.dma_start(out=out[i * P : (i + 1) * P, :], in_=res[:])
 
+        def out_product(i):
+            bank = next_scalar_bank()
+            out_passes(bank, i, 0, CHUNKS)
+            store(bank, i)
+
         def subtract(i, lo, hi):
             g = lo // CHUNK
             nc.vector.tensor_tensor(out=diff[i % 2][:, lo:hi], in0=pred_banks[g][:, lo - g * CHUNK : hi - g * CHUNK],
-                                    in1=y_ring[i % RING_IN][:, lo:hi], op=SUB)
+                                    in1=y_ring[i % RING_IN][:, lo:hi], op=mybir.AluOpType.subtract)
 
-        def weigh(engine, i, lo, hi):
-            target = e_tile(i, lo // CHUNK)[:].rearrange("p (h q r) -> p q h r", h=2, r=RUN)
-            base = lo - lo % (N // 2)
+        def weigh(engine, i, first, count):
+            lo, hi = first * CHUNK, (first + count) * CHUNK
+            blocks = slice((first % 2) * CHUNK // (2 * RUN), (first % 2 + count) * CHUNK // (2 * RUN))
             engine.tensor_tensor(
-                out=target[:, (lo - base) // BLOCK : (hi - base) // BLOCK, :, :],
+                out=e_tile(i, first)[:].rearrange("p (h q r) -> p q h r", h=2, r=RUN)[:, blocks, :, :],
                 in0=diff[i % 2][:, lo:hi].rearrange("p (q h r) -> p q h r", h=2, r=RUN),
                 in1=mask_ring[i % RING_IN][:, lo:hi].rearrange("p (q h r) -> p q h r", h=2, r=RUN),
-                op=MULT,
+                op=mybir.AluOpType.mult,
             )
-
-        def quantise_e(i, first=0, count=CHUNKS):
-            quantise(e_mx[i % 6], stage_of(("e", i))[:, first * CHUNK : (first + count) * CHUNK], first * P)
 
         def load_y(i, lo, hi):
             nc.sync.dma_start(out=y_ring[i % RING_IN][:, lo:hi], in_=y[i * P : (i + 1) * P, lo:hi])
@@ -197,122 +216,112 @@ def tile_scaled_completion_gradient_s11_kernel(tc, u, v_words, v_scales, c, y, m
             load_mask(i)
 
         def load_u(k):
-            a, b = u_loads[k]
-            nc.sync.dma_start(out=u_raw[k][:].rearrange("p (t k) -> p t k", k=R),
-                              in_=u[a * P : b * P, :].rearrange("(t p) k -> p t k", p=P))
+            a, b = U_LOADS[k]
+            nc.sync.dma_start(out=u_raw[k][:].rearrange("p (s k) -> p s k", k=R),
+                              in_=u[a * P : b * P, :].rearrange("(s p) k -> p s k", p=P))
 
         def load_v(half):
             nc.sync.dma_start(out=v_codes[half][:].bitcast(I32),
                               in_=v_words[0, :, half * N : (half + 1) * N].bitcast(I32))
 
-        def load_c():
-            nc.sync.dma_start(out=c_raw[:], in_=c.rearrange("(p t) j -> p t j", t=4))
-
-        nc.vector.memset(v_plane[:].bitcast(I32), 0)
+        nc.gpsimd.memset(v_plane[:].bitcast(I32), 0)
         make_identity(nc, ident[:])
         load_u(0)
         for r in range(4):
             nc.sync.dma_start(out=v_plane[r:P:32, :].bitcast(I32), in_=v_scales[0, r:16:4, :].bitcast(I32))
+        nc.sync.dma_start(out=c_raw[:], in_=c.rearrange("(p t) j -> p t j", t=PACK))
         load_v(0)
-        load_y(0, 0, N // 2)
-        load_u(1)
-        load_c()
+        load_y(0, 0, HALF)
         load_v(1)
-        load_y(0, N // 2, N)
-        load_u(2)
+        load_u(1)
+        load_y(0, HALF, N)
         load_mask(0)
-        load_y(1, 0, N)
-        load_mask(1)
-        load_u(3)
+        load_tile(1)
+        load_u(2)
         load_tile(2)
         load_tile(3)
-        load_u(4)
+        load_u(3)
         for i in range(4, RING_IN):
             load_tile(i)
 
-        c_sorted = stage_of(("c", 0))[:].rearrange("p (j t) -> p j t", t=4)
+        c_sorted = staged[("c", 0)].rearrange("p (j t) -> p j t", t=PACK)
         c_source = c_raw[:].rearrange("p t j -> p j t")
         turn_u(0)
-        quantise(u_mx[0], u_stage[0][:])
-        def job(kind, k):
-            if kind == "tu":
-                turn_u(k)
-            elif kind == "tz":
-                turn_z(k)
-            elif kind == "te":
-                turn_e(k, 0, 2)
-                turn_e(k, 2, 2)
-            elif kind == "z":
-                z_product(k)
-            elif kind == "o":
-                out_product(k)
-            elif kind == "qu":
-                quantise(u_mx[k], u_stage[k % 4][:])
-            elif kind == "qc":
-                quantise(c_mx[0], stage_of(("c", 0))[:])
-            elif kind == "qz":
-                quantise(z_mx[k], stage_of(("z", k))[:])
-            elif kind == "qe":
-                quantise_e(k)
-            elif kind == "cv":
-                nc.vector.tensor_copy(out=c_sorted[:, 0 : R // 2, :], in_=c_source[:, 0 : R // 2, :])
-
-        predict(0, 0)
-        predict(0, 1)
+        quantise_call(calls_of["head"][0])
         turn_u(1)
-        predict(0, 2)
-        predict(0, 3)
-        nc.scalar.copy(out=c_sorted[:, R // 2 : R, :], in_=c_source[:, R // 2 : R, :])
+        nc.vector.tensor_copy(out=c_sorted[:, 0:C_VECTOR, :], in_=c_source[:, 0:C_VECTOR, :])
+        nc.scalar.copy(out=c_sorted[:, C_VECTOR:R, :], in_=c_source[:, C_VECTOR:R, :])
+        quantise_call(calls_of["head"][1])
+        quantise_call(calls_of["head"][2])
+        for g in range(CHUNKS):
+            predict(0, g)
         turn_u(2)
-        turn_u(3)
+        z_product(0)
 
-        split = N - GPSIMD_COLUMNS
-        gate = N - GATE_COLUMNS
-        for i in range(TILES - 1):
+        for i in range(LAST):
             for g in range(CHUNKS):
-                subtract(i, g * CHUNK, min((g + 1) * CHUNK, gate))
-                if i == 0 and g == 1:
-                    job("cv", 0)
-                    job("qu", 1)
-                    predict(1, 0)
-                if g < CHUNKS - 1 and (i, g) != (0, 0):
+                subtract(i, g * CHUNK, min((g + 1) * CHUNK, N - GATE))
+                if g < CHUNKS - 1:
                     predict(i + 1, g)
-            for kind, k in QUANTS.get(i, []) + MID.get(i, []):
-                job(kind, k)
-            if split > N // 2:
-                weigh(nc.vector, i, N // 2, split)
-            if i < TILES - 2 and i not in LATEQ:
-                subtract(i, gate, N)
-                weigh(nc.vector, i, 0, N // 2)
+            late = i in (0, LAST - 1)
+            for call in calls_of.get(i, []) if i > 0 else []:
+                quantise_call(call)
+            for k in range(LAST - 2):
+                if e_step(k) - 1 == i:
+                    turn_e(k, 0, 2)
+                    turn_e(k, 2, 2)
+            if i == LAST - 1:
+                turn_e(i - 1, 0, 2)
+                turn_e(i - 1, 2, 2)
+            ready = [k for k in range(LAST - 2) if e_step(k) == i]
+            early = ready[:1] if i > Z_DONE else []
+            for k in early:
+                out_product(k)
+            if not late:
+                subtract(i, N - GATE, N)
+                weigh(nc.vector, i, 0, 2)
             else:
-                weigh(nc.vector, i, 0, N // 2)
-                for kind, k in LATEQ.get(i, []):
-                    job(kind, k)
-                subtract(i, gate, N)
-            weigh(nc.gpsimd, i, split, N)
+                weigh(nc.vector, i, 0, 2)
+                quantise_call(calls_of[0][0] if i == 0 else calls_of["tail"][0])
+                subtract(i, N - GATE, N)
+            weigh(nc.gpsimd, i, 2, 2)
             predict(i + 1, CHUNKS - 1)
-            for kind, k in LATE.get(i, []):
-                job(kind, k)
+            if i in U_TURNS:
+                turn_u(U_TURNS[i])
+            if i < CHUNKS:
+                turn_z(i)
+            if i < CHUNKS - 1:
+                z_product(i + 1)
+            for k in ready[len(early) :]:
+                out_product(k)
             if i + RING_IN < TILES:
                 load_tile(i + RING_IN)
 
-        i = TILES - 1
-        turn_e(i - 1, 0, 2)
-        out_product(i - 2)
+        turn_e(LAST - 1, 0, 2)
+        out_product(LAST - 2)
         for g in range(CHUNKS):
-            subtract(i, g * CHUNK, (g + 1) * CHUNK)
-        turn_e(i - 1, 2, 2)
-        quantise_e(i - 1, 0, 2)
-        out_product(i - 1, 0, 2)
-        weigh(nc.vector, i, 0, 2 * CHUNK)
-        turn_e(i, 0, 2)
-        quantise_e(i - 1, 2, 2)
-        out_product(i - 1, 2, 2)
-        weigh(nc.vector, i, 2 * CHUNK, 3 * CHUNK)
-        turn_e(i, 2, 1)
-        weigh(nc.vector, i, 3 * CHUNK, N)
-        turn_e(i, 3, 1)
-        quantise_e(i, 0, 2)
-        quantise_e(i, 2, 1)
-        quantise_e(i, 3, 1)
-        out_product(i)
+            subtract(LAST, g * CHUNK, (g + 1) * CHUNK)
+        turn_e(LAST - 1, 2, 2)
+        before = next_scalar_bank()
+        quantise_e(LAST - 1, 0, 2)
+        out_passes(before, LAST - 1, 0, 2)
+        weigh(nc.vector, LAST, 0, 2)
+        turn_e(LAST, 0, 2)
+        quantise_e(LAST - 1, 2, 2)
+        out_passes(before, LAST - 1, 2, 2)
+        store(before, LAST - 1)
+        weigh(nc.vector, LAST, 2, 1)
+        turn_e(LAST, 2, 1)
+        weigh(nc.vector, LAST, 3, 1)
+        turn_e(LAST, 3, 1)
+        quantise_e(LAST, 0, 2)
+        quantise_e(LAST, 2, 1)
+        quantise_e(LAST, 3, 1)
+        res = result[LAST % RING_OUT]
+        for g in range(CHUNKS):
+            for half in range(2):
+                out_passes(pred_banks[half], LAST, g, 1, half * R // 2, (half + 1) * R // 2)
+        nc.scalar.copy(out=res[:, 0 : R // 2], in_=pred_banks[0][:, 0 : R // 2])
+        nc.scalar.dma_start(out=out[LAST * P : M, 0 : R // 2], in_=res[:, 0 : R // 2])
+        nc.vector.tensor_copy(out=res[:, R // 2 : R], in_=pred_banks[1][:, 0 : R // 2])
+        nc.sync.dma_start(out=out[LAST * P : M, R // 2 : R], in_=res[:, R // 2 : R])

from contextlib import ExitStack

import concourse.mybir as mybir
from concourse.masks import make_identity

M, N, R = 1536, 2048, 512
FLOPS = 2 * M * N * R + 2 * N * R * R + 2 * M * N * R

F32 = mybir.dt.float32
BF16 = mybir.dt.bfloat16
I32 = mybir.dt.int32
U32 = mybir.dt.uint32
U8 = mybir.dt.uint8
FP8X4 = mybir.dt.float8_e4m3fn_x4
FP4X4 = mybir.dt.float4_e2m1fn_x4

P = 128
PACK = 4
CHUNK = 512
TILES = M // P
CHUNKS = N // CHUNK
HALF = N // 2
RUN = 16
LAST = TILES - 1

GATE = 64
U_GROUPS = [(0, 1), (1, 2), (2, 4), (4, 8), (8, 12)]
U_LOADS = [(0, 2), (2, 4), (4, 8), (8, 12)]
C_VECTOR = 320
U_TURNS = {1: 3, 5: 4}
Z_DONE = CHUNKS

RING_IN = 8
RING_E = 4
RING_OUT = 4
RING_STAGE = 5
WIDEST = 2 * N


def e_step(k):
    return max(k + 2, Z_DONE + (k + 1) // 2)


def tile_scaled_completion_gradient_s11_kernel(tc, u, v_words, v_scales, c, y, mask, out):
    nc = tc.nc

    with ExitStack() as ctx:
        keep = ctx.enter_context(tc.tile_pool(name="keep", bufs=1))
        psum = ctx.enter_context(tc.psum_pool(name="psum", bufs=1))
        ctx.enter_context(tc.manual_schedule())

        def tiles(name, count, shape, dtype):
            return [keep.tile(shape, dtype, name="%s%d" % (name, k), align_bytes=64) for k in range(count)]

        banks = [psum.tile([P, CHUNK], F32, name="bank%d" % k) for k in range(8)]
        pred_banks, scalar_banks = banks[:CHUNKS], banks[CHUNKS:]
        scalar_bank_uses = []

        def next_scalar_bank():
            scalar_bank_uses.append(None)
            return scalar_banks[len(scalar_bank_uses) % len(scalar_banks)]

        ident = keep.tile([P, P], F32, name="ident", align_bytes=64)
        v_plane = keep.tile([P, N], U8, name="v_plane", align_bytes=64)
        v_codes = tiles("v_codes", 2, [P, N], U8)
        c_raw = keep.tile([P, PACK, R], BF16, name="c_raw", align_bytes=64)
        u_raw = [keep.tile([P, (b - a) * R], BF16, name="u_raw%d" % a, align_bytes=64) for a, b in U_LOADS]
        y_ring = tiles("y", RING_IN, [P, N], BF16)
        mask_ring = tiles("mask", RING_IN, [P, N], BF16)
        diff = tiles("diff", 2, [P, N], F32)
        e_sorted = [tiles("e_sorted%d_" % k, 2, [P, HALF], BF16) for k in range(RING_E)]
        z_sorted = tiles("z_sorted", 2 * PACK, [P, CHUNK], BF16)
        stage = tiles("stage", RING_STAGE, [P, WIDEST], BF16)
        result = tiles("result", RING_OUT, [P, R], F32)

        def width_of(operand):
            kind, k = operand
            return (U_GROUPS[k][1] - U_GROUPS[k][0]) * R if kind == "u" else N

        calls_of = {"head": [[("u", 0)], [("u", 1)], [("c", 0)]], 0: [[("u", 2)]],
                    1: [[("z", 0)]], 2: [[("u", 3)]], 3: [[("z", 1), ("z", 2)]]}
        for step in range(Z_DONE, LAST):
            calls_of[step] = [[("z", CHUNKS - 1)] * (step == Z_DONE) + [("e", k) for k in range(TILES) if e_step(k) == step]]
        calls_of[6].append([("u", 4)])
        calls_of["tail"] = [[("e", k)] for k in range(LAST - 2, TILES)]

        staged, codes_of, scales_of, whole_call = {}, {}, {}, {}
        order = ["head"] + [step for step in range(LAST) if step in calls_of] + ["tail"]
        for number, call in enumerate([call for step in order for call in calls_of[step]]):
            width = sum(width_of(operand) for operand in call)
            codes = keep.tile([P, width // PACK], U32, name="codes%d" % number, align_bytes=64)
            scales = keep.tile([P, width // PACK], U8, name="scales%d" % number, align_bytes=64)
            source = stage[number % RING_STAGE]
            whole_call[call[0]] = (codes[:], scales[:], source[:, 0:width])
            at = 0
            for operand in call:
                end = at + width_of(operand)
                staged[operand] = source[:, at:end]
                codes_of[operand] = codes[:, at // PACK : end // PACK]
                scales_of[operand] = scales[:, at // PACK : end // PACK]
                at = end

        def quantise(codes, scales, source):
            nc.vector.quantize_mx(out=codes.bitcast(FP8X4), scales=scales, in_=source)

        def quantise_call(call):
            quantise(*whole_call[call[0]])

        def quantise_e(k, first, count):
            words = slice(first * P, (first + count) * P)
            quantise(codes_of[("e", k)][:, words], scales_of[("e", k)][:, words],
                     staged[("e", k)][:, first * CHUNK : (first + count) * CHUNK])

        def columns(operand, start, width):
            return (codes_of[operand][:, start : start + width].bitcast(FP8X4), scales_of[operand][:, start : start + width])

        def u_columns(i):
            k = [a <= i < b for a, b in U_GROUPS].index(True)
            return columns(("u", k), (i - U_GROUPS[k][0]) * P, P)

        def v_columns(g):
            codes = v_codes[g // 2][:, (g % 2) * 2 * CHUNK : (g % 2 + 1) * 2 * CHUNK]
            return (codes.bitcast(FP4X4), v_plane[:, g * CHUNK : (g + 1) * CHUNK])

        def mx(target, stationary, moving, start=True, stop=True):
            nc.tensor.matmul_mx(out=target, lhsT=stationary[0], lhsT_scale=stationary[1],
                                rhs=moving[0], rhs_scale=moving[1], start=start, stop=stop)

        def turn(halves, target):
            bank = next_scalar_bank()
            for k, words in enumerate(halves):
                nc.tensor.transpose(bank[:, k * P : (k + 1) * P], words, ident[:])
            sets = len(halves) // 2
            nc.scalar.copy(
                out=target.bitcast(F32).rearrange("p (s m h) -> p s m h", s=sets, h=2),
                in_=bank[:, 0 : sets * 2 * P].rearrange("p (s h m) -> p s m h", s=sets, h=2),
            )

        def turn_u(k):
            a, b = U_GROUPS[k]
            load = [lo <= a < hi for lo, hi in U_LOADS].index(True)
            words = u_raw[load][:].bitcast(F32)
            for first in range(a, b, 2):
                sets = [s - U_LOADS[load][0] for s in range(first, min(first + 2, b))]
                halves = [words[:, s * R // 2 + h : (s + 1) * R // 2 : 2] for s in sets for h in range(2)]
                turn(halves, staged[("u", k)][:, (first - a) * R : (first - a + len(sets)) * R])

        def sorted_halves(tile, sets, s):
            words = tile[:].bitcast(F32)
            return [words[:, (h * sets + s) * P : (h * sets + s + 1) * P] for h in range(2)]

        def e_tile(i, g):
            if i == LAST and g == CHUNKS - 1:
                return e_sorted[(i + 1) % RING_E][1]
            return e_sorted[i % RING_E][g // 2]

        def turn_e(i, first, count):
            halves = [w for g in range(first, first + count) for w in sorted_halves(e_tile(i, g), 2, g % 2)]
            turn(halves, staged[("e", i)][:, first * CHUNK : (first + count) * CHUNK])

        def turn_z(g):
            for first in (0, 2):
                halves = [w for j in (first, first + 1) for w in sorted_halves(z_sorted[(g % 2) * PACK + j], 1, 0)]
                turn(halves, staged[("z", g)][:, first * CHUNK : (first + 2) * CHUNK])

        def predict(i, g):
            mx(pred_banks[g][:], u_columns(i), v_columns(g))

        def z_product(g):
            for j in range(R // P):
                bank = next_scalar_bank()
                mx(bank[:], columns(("c", 0), j * P, P), v_columns(g))
                nc.scalar.copy(
                    out=z_sorted[(g % 2) * PACK + j][:].rearrange("p (h q r) -> p h q r", h=2, r=RUN),
                    in_=bank[:].rearrange("p (q h r) -> p h q r", h=2, r=RUN),
                )

        def out_passes(bank, i, first, count, lo=0, hi=R):
            for g in range(first, first + count):
                mx(bank[:, 0 : hi - lo], columns(("e", i), g * P, P), columns(("z", g), lo, hi - lo),
                   start=(g == 0), stop=(g == CHUNKS - 1))

        def store(bank, i):
            res = result[i % RING_OUT]
            nc.scalar.copy(out=res[:], in_=bank[:])
            nc.sync.dma_start(out=out[i * P : (i + 1) * P, :], in_=res[:])

        def out_product(i):
            bank = next_scalar_bank()
            out_passes(bank, i, 0, CHUNKS)
            store(bank, i)

        def subtract(i, lo, hi):
            g = lo // CHUNK
            nc.vector.tensor_tensor(out=diff[i % 2][:, lo:hi], in0=pred_banks[g][:, lo - g * CHUNK : hi - g * CHUNK],
                                    in1=y_ring[i % RING_IN][:, lo:hi], op=mybir.AluOpType.subtract)

        def weigh(engine, i, first, count):
            lo, hi = first * CHUNK, (first + count) * CHUNK
            blocks = slice((first % 2) * CHUNK // (2 * RUN), (first % 2 + count) * CHUNK // (2 * RUN))
            engine.tensor_tensor(
                out=e_tile(i, first)[:].rearrange("p (h q r) -> p q h r", h=2, r=RUN)[:, blocks, :, :],
                in0=diff[i % 2][:, lo:hi].rearrange("p (q h r) -> p q h r", h=2, r=RUN),
                in1=mask_ring[i % RING_IN][:, lo:hi].rearrange("p (q h r) -> p q h r", h=2, r=RUN),
                op=mybir.AluOpType.mult,
            )

        def load_y(i, lo, hi):
            nc.sync.dma_start(out=y_ring[i % RING_IN][:, lo:hi], in_=y[i * P : (i + 1) * P, lo:hi])

        def load_mask(i):
            nc.sync.dma_start(out=mask_ring[i % RING_IN][:], in_=mask[i * P : (i + 1) * P, :])

        def load_tile(i):
            load_y(i, 0, N)
            load_mask(i)

        def load_u(k):
            a, b = U_LOADS[k]
            nc.sync.dma_start(out=u_raw[k][:].rearrange("p (s k) -> p s k", k=R),
                              in_=u[a * P : b * P, :].rearrange("(s p) k -> p s k", p=P))

        def load_v(half):
            nc.sync.dma_start(out=v_codes[half][:].bitcast(I32),
                              in_=v_words[0, :, half * N : (half + 1) * N].bitcast(I32))

        nc.gpsimd.memset(v_plane[:].bitcast(I32), 0)
        make_identity(nc, ident[:])
        load_u(0)
        for r in range(4):
            nc.sync.dma_start(out=v_plane[r:P:32, :].bitcast(I32), in_=v_scales[0, r:16:4, :].bitcast(I32))
        nc.sync.dma_start(out=c_raw[:], in_=c.rearrange("(p t) j -> p t j", t=PACK))
        load_v(0)
        load_y(0, 0, HALF)
        load_v(1)
        load_u(1)
        load_y(0, HALF, N)
        load_mask(0)
        load_tile(1)
        load_u(2)
        load_tile(2)
        load_tile(3)
        load_u(3)
        for i in range(4, RING_IN):
            load_tile(i)

        c_sorted = staged[("c", 0)].rearrange("p (j t) -> p j t", t=PACK)
        c_source = c_raw[:].rearrange("p t j -> p j t")
        turn_u(0)
        quantise_call(calls_of["head"][0])
        turn_u(1)
        nc.vector.tensor_copy(out=c_sorted[:, 0:C_VECTOR, :], in_=c_source[:, 0:C_VECTOR, :])
        nc.scalar.copy(out=c_sorted[:, C_VECTOR:R, :], in_=c_source[:, C_VECTOR:R, :])
        quantise_call(calls_of["head"][1])
        quantise_call(calls_of["head"][2])
        for g in range(CHUNKS):
            predict(0, g)
        turn_u(2)
        z_product(0)

        for i in range(LAST):
            for g in range(CHUNKS):
                subtract(i, g * CHUNK, min((g + 1) * CHUNK, N - GATE))
                if g < CHUNKS - 1:
                    predict(i + 1, g)
            late = i in (0, LAST - 1)
            for call in calls_of.get(i, []) if i > 0 else []:
                quantise_call(call)
            for k in range(LAST - 2):
                if e_step(k) - 1 == i:
                    turn_e(k, 0, 2)
                    turn_e(k, 2, 2)
            if i == LAST - 1:
                turn_e(i - 1, 0, 2)
                turn_e(i - 1, 2, 2)
            ready = [k for k in range(LAST - 2) if e_step(k) == i]
            early = ready[:1] if i > Z_DONE else []
            for k in early:
                out_product(k)
            if not late:
                subtract(i, N - GATE, N)
                weigh(nc.vector, i, 0, 2)
            else:
                weigh(nc.vector, i, 0, 2)
                quantise_call(calls_of[0][0] if i == 0 else calls_of["tail"][0])
                subtract(i, N - GATE, N)
            weigh(nc.gpsimd, i, 2, 2)
            predict(i + 1, CHUNKS - 1)
            if i in U_TURNS:
                turn_u(U_TURNS[i])
            if i < CHUNKS:
                turn_z(i)
            if i < CHUNKS - 1:
                z_product(i + 1)
            for k in ready[len(early) :]:
                out_product(k)
            if i + RING_IN < TILES:
                load_tile(i + RING_IN)

        turn_e(LAST - 1, 0, 2)
        out_product(LAST - 2)
        for g in range(CHUNKS):
            subtract(LAST, g * CHUNK, (g + 1) * CHUNK)
        turn_e(LAST - 1, 2, 2)
        before = next_scalar_bank()
        quantise_e(LAST - 1, 0, 2)
        out_passes(before, LAST - 1, 0, 2)
        weigh(nc.vector, LAST, 0, 2)
        turn_e(LAST, 0, 2)
        quantise_e(LAST - 1, 2, 2)
        out_passes(before, LAST - 1, 2, 2)
        store(before, LAST - 1)
        weigh(nc.vector, LAST, 2, 1)
        turn_e(LAST, 2, 1)
        weigh(nc.vector, LAST, 3, 1)
        turn_e(LAST, 3, 1)
        quantise_e(LAST, 0, 2)
        quantise_e(LAST, 2, 1)
        quantise_e(LAST, 3, 1)
        res = result[LAST % RING_OUT]
        for g in range(CHUNKS):
            for half in range(2):
                out_passes(pred_banks[half], LAST, g, 1, half * R // 2, (half + 1) * R // 2)
        nc.scalar.copy(out=res[:, 0 : R // 2], in_=pred_banks[0][:, 0 : R // 2])
        nc.scalar.dma_start(out=out[LAST * P : M, 0 : R // 2], in_=res[:, 0 : R // 2])
        nc.vector.tensor_copy(out=res[:, R // 2 : R], in_=pred_banks[1][:, 0 : R // 2])
        nc.sync.dma_start(out=out[LAST * P : M, R // 2 : R], in_=res[:, R // 2 : R])
